import numpy as np
import ml_dtypes


def mxq(x, axis, fmt="e4m3"):
    dtype, down = {"e4m3": (ml_dtypes.float8_e4m3fn, 7), "e5m2": (ml_dtypes.float8_e5m2, 14)}[fmt]
    v = np.moveaxis(np.asarray(x, np.float32).astype(ml_dtypes.bfloat16).astype(np.float64), axis, -1)
    blocks = v.reshape(v.shape[:-1] + (-1, 32))
    amax = np.abs(blocks).max(-1, keepdims=True)
    byte = np.maximum(np.where(amax > 0, np.frexp(amax)[1] - 1 + 127, 0) - down, 1)
    scale = np.exp2(byte - 127.0)
    codes = (blocks / scale).astype(np.float32).astype(dtype).astype(np.float64)
    return np.moveaxis((codes * scale).reshape(v.shape), -1, axis)


WIDE = False


def mx_kscale(k):
    if not WIDE:
        return np.ones(k)
    levels = np.array([10, -10, 5, -5, 0])
    if k % 512:
        return np.exp2(np.random.permutation(np.resize(levels, k // 32))).repeat(32)
    a = np.empty((k // 512, 16))
    for p in range(k // 512):
        a[p, :8] = np.random.permutation(np.resize(levels, 8))
        for g in range(8):
            far = levels[np.abs(levels - a[p, g]) >= 10]
            a[p, g + 8] = far[np.random.randint(len(far))]
    return np.exp2(a.ravel()).repeat(32)


def f64(x):
    return np.asarray(x).astype(np.float64)


def striped(idx):
    return np.tile(np.asarray(idx).reshape(-1, 16).T, (8, 1)).astype(np.uint16)


def unstriped(offs):
    return offs[:16].T.reshape(-1).astype(np.int64)


E2M1 = np.array([0.0, 0.5, 1.0, 1.5, 2.0, 3.0, 4.0, 6.0, -0.0, -0.5, -1.0, -1.5, -2.0, -3.0, -4.0, -6.0])


def pack_weight(w, fmt):
    k, n = w.shape
    w = f64(np.asarray(w, np.float32).astype(ml_dtypes.bfloat16)).reshape(k // 32, 32, n)
    amax = np.abs(w).max(1)
    if fmt == "e4m3":
        byte = np.frexp(amax)[1] - 1 + 127 - 7
    else:
        mant, ex = np.frexp(amax / 6.0)
        byte = np.where(mant > 0.5, ex, ex - 1) + 127
    byte = np.clip(np.where(amax > 0, byte, 1), 1, 254)
    scaled = (w * np.exp2(127.0 - byte)[:, None, :]).reshape(k, n).astype(np.float32)
    by_word = np.ascontiguousarray(scaled.reshape(k // 512, 128, 4, n).transpose(0, 1, 3, 2))
    if fmt == "e4m3":
        words = by_word.astype(ml_dtypes.float8_e4m3fn).view(np.uint8)
    else:
        c = by_word.astype(ml_dtypes.float4_e2m1fn).view(np.uint8) & 0xF
        words = (c[..., 0::2] | (c[..., 1::2] << 4)).reshape(k // 512, 128, 2 * n)
    return np.ascontiguousarray(words), np.ascontiguousarray(byte.astype(np.uint8).reshape(k // 512, 16, n))


def unpack_weight(words, scales, fmt):
    g, _, n = scales.shape
    words = np.ascontiguousarray(words).reshape(g, 128, n, -1)
    if fmt == "e4m3":
        vals = words.view(ml_dtypes.float8_e4m3fn).astype(np.float64)
    else:
        nib = np.empty((g, 128, n, 4), np.uint8)
        nib[..., 0::2] = words & 0xF
        nib[..., 1::2] = words >> 4
        vals = E2M1[nib]
    vals = vals * np.repeat(np.exp2(scales.astype(np.float64) - 127.0), 8, axis=1)[..., None]
    return vals.transpose(0, 1, 3, 2).reshape(g * 512, n)


D, E, T, I, Q, G = 512, 512, 2048, 512, 128, 64


def setup_inputs():
    n = np.random.standard_normal
    idx = np.random.permutation(T)[:I]
    fd = mx_kscale(D)
    fe = mx_kscale(E)
    keysp = pack_weight(n((D, T)) / fd[:, None], "e2m1")
    valsp = pack_weight(n((E, T)) / fe[:, None], "e2m1")
    return {
        "query": (n((D, Q)) * 0.7 / np.sqrt(D) * fd[:, None]).astype(np.float32),
        "keys_words": keysp[0],
        "keys_scales": keysp[1],
        "share": (np.random.uniform(0.2, 0.8, (Q, 1))).astype(np.float32),
        "gout": (n((E, Q)) * 1 / np.sqrt(E) * fe[:, None]).astype(np.float32),
        "vals_words": valsp[0],
        "vals_scales": valsp[1],
        "old": (0.5 * n((Q, T))).astype(np.float32),
        "offs": striped(idx),
    }


def reference(query, keys_words, keys_scales, share, gout, vals_words, vals_scales, old, offs):
    idx = unstriped(offs)
    keysu = unpack_weight(keys_words, keys_scales, "e2m1")
    valsu = unpack_weight(vals_words, vals_scales, "e2m1")
    queryq = mxq(f64(query), 0, "e4m3")
    keysidxg = keysu[:, idx]
    a = queryq.T @ keysidxg
    p = np.exp(a)
    z = np.sum(p, axis=1, keepdims=True)
    s = p.reshape(Q, G, I // G).sum(axis=2)
    v1 = 1.0 / (z * f64(share) + s * (1.0 - f64(share)) * 64.0)
    vr = np.repeat(v1, I // G, axis=1)
    goutq = mxq(f64(gout), 0, "e4m3")
    valsidxg = valsu[:, idx]
    c0 = goutq.T @ valsidxg
    dvr = c0 * p
    dv1 = dvr.reshape(Q, G, I // G).sum(axis=2)
    ds = dv1 * (-1.0) / np.square(z * f64(share) + s * (1.0 - f64(share)) * 64.0) * 64.0 * (1.0 - f64(share))
    r1 = np.repeat(ds, I // G, axis=1)
    dz = np.sum(dv1 * (-1.0) / np.square(z * f64(share) + s * (1.0 - f64(share)) * 64.0), axis=1, keepdims=True) * f64(share)
    dp = c0 * vr + r1 + dz
    da = dp * p
    gs = da * 512.0
    gf = np.zeros((Q, T))
    gf[:, idx] = gs
    y = f64(old) + gf
    return y

@@ -1,0 +1,181 @@
+from contextlib import ExitStack
+
+import concourse.mybir as mybir
+
+D, E, T, SLOTS, Q, GROUPS = 512, 512, 2048, 512, 128, 64
+GROUP = SLOTS // GROUPS
+P = 128
+PACK = 4
+FLOPS = 2 * Q * SLOTS * (D + E)
+
+F32 = mybir.dt.float32
+BF16 = mybir.dt.bfloat16
+I32 = mybir.dt.int32
+U32 = mybir.dt.uint32
+U16 = mybir.dt.uint16
+U8 = mybir.dt.uint8
+FP8X4 = mybir.dt.float8_e4m3fn_x4
+FP4X4 = mybir.dt.float4_e2m1fn_x4
+ALU = mybir.AluOpType
+ACT = mybir.ActivationFunctionType
+AXIS = mybir.AxisListType
+
+OUT_SCALE = 512.0
+GROUP_WEIGHT = 64.0
+SOFT = 4.0
+LN2 = 0.6931471805599453
+HALF = SLOTS // 2
+STORE_WIDTHS = (256, 256, 512, 512, 512)
+
+
+def tile_attend_bmixednorm_s_kernel(tc, query, keys_words, keys_scales, share, gout, vals_words, vals_scales, old, offs, out):
+    nc = tc.nc
+    with ExitStack() as ctx:
+        sb = ctx.enter_context(tc.tile_pool(name="sb", bufs=1))
+        psum = ctx.enter_context(tc.psum_pool(name="psum", bufs=1))
+
+        offsets = sb.tile([P, SLOTS // 16], U16, name="offsets")
+        nc.sync.dma_start(offsets[:], offs)
+
+        def load_words(name, words):
+            word_pool = sb.tile([P, T], U16, name=name + "_word_pool", tag=name + "_word_pool", align_bytes=64)
+            nc.sync.dma_start(word_pool[:].bitcast(I32), words[0].bitcast(I32))
+            return word_pool
+
+        def load_scales(name, scales):
+            scale_pool = sb.tile([P, T], U8, name=name + "_scale_pool", tag=name + "_scale_pool", align_bytes=64)
+            nc.vector.memset(scale_pool[:].bitcast(I32), 0)
+            for quadrant in range(4):
+                nc.sync.dma_start(
+                    scale_pool[32 * quadrant : 32 * quadrant + 4, :].bitcast(I32),
+                    scales[0, 4 * quadrant : 4 * quadrant + 4, :].bitcast(I32),
+                )
+            return scale_pool
+
+        def load_rows(name, rows):
+            raw = sb.tile([P, PACK, Q], F32, name=name + "_raw", tag="raw")
+            nc.sync.dma_start(raw[:], rows.rearrange("(p j) q -> p j q", j=PACK))
+            return raw
+
+        def quantise(name, raw):
+            grouped = sb.tile([P, Q, PACK], BF16, name=name + "_grouped", tag=name + "_grouped", align_bytes=64)
+            nc.scalar.copy(grouped[:], raw[:].rearrange("p j q -> p q j"))
+            codes = sb.tile([P, Q], U32, name=name + "_codes", align_bytes=64)
+            code_scales = sb.tile([P, Q], U8, name=name + "_code_scales", align_bytes=64)
+            nc.vector.quantize_mx(
+                out=codes[:].bitcast(FP8X4), scales=code_scales[:], in_=grouped[:].rearrange("p q j -> p (q j)")
+            )
+            return codes, code_scales
+
+        def gather(name, pool, dtype):
+            listed = sb.tile([P, SLOTS], dtype, name=name, align_bytes=64)
+            nc.vector.tensor_copy(listed[:], pool[:].indirect(offsets[:]))
+            return listed
+
+        def product(name, codes, code_scales, words, scales):
+            bank = psum.tile([P, SLOTS], F32, name=name + "_bank")
+            nc.tensor.matmul_mx(
+                out=bank[:],
+                lhsT=codes[:].bitcast(FP8X4),
+                lhsT_scale=code_scales[:],
+                rhs=words[:].bitcast(FP4X4),
+                rhs_scale=scales[:],
+                start=True,
+                stop=True,
+            )
+            return bank
+
+        key_word_pool = load_words("key", keys_words)
+        key_scale_pool = load_scales("key", keys_scales)
+        share_col = sb.tile([P, 1], F32, name="share_col", tag="val_word_pool", align_bytes=64)
+        nc.sync.dma_start(share_col[:], share)
+        query_raw = load_rows("query", query)
+        val_scale_pool = load_scales("val", vals_scales)
+
+        warm = sb.tile([P, 1], F32, name="warm")
+        nc.vector.memset(warm[:], 0.0)
+        nc.scalar.activation(warm[:], warm[:], ACT.Exp)
+
+        group_factor = sb.tile([P, 1], F32, name="group_factor")
+        neg_group_factor = sb.tile([P, 1], F32, name="neg_group_factor")
+        neg_row_factor = sb.tile([P, 1], F32, name="neg_row_factor")
+        ratio = GROUP_WEIGHT / OUT_SCALE
+        nc.scalar.activation(group_factor[:], share_col[:], ACT.Copy, scale=-ratio, bias=ratio)
+        nc.scalar.activation(neg_group_factor[:], share_col[:], ACT.Copy, scale=ratio, bias=-ratio)
+        nc.scalar.activation(neg_row_factor[:], share_col[:], ACT.Copy, scale=-1.0 / OUT_SCALE)
+
+        val_word_pool = load_words("val", vals_words)
+        placed = sb.tile([P, T], F32, name="placed")
+        nc.vector.memset(placed[:], 0.0)
+
+        key_words = gather("key_words", key_word_pool, U16)
+        key_scales = gather("key_scales", key_scale_pool, U8)
+        query_codes, query_scales = quantise("query", query_raw)
+        a = product("score", query_codes, query_scales, key_words, key_scales)
+
+        gout_raw = load_rows("gout", gout)
+        val_scales = gather("val_scales", val_scale_pool, U8)
+        gout_codes, gout_scales = quantise("gout", gout_raw)
+        val_words = gather("val_words", val_word_pool, U16)
+        c0 = product("back", gout_codes, gout_scales, val_words, val_scales)
+
+        result = sb.tile([P, T], F32, name="result", tag="val_scale_pool", align_bytes=64)
+        nc.sync.dma_start(result[:], old)
+
+        p = sb.tile([P, SLOTS], F32, name="p")
+        soft_sum = sb.tile([P, 1], F32, name="soft_sum")
+        neg_shift = sb.tile([P, 1], F32, name="neg_shift")
+        nc.scalar.activation(p[:], a[:], ACT.Exp, scale=1.0 / SOFT, accum_out=soft_sum[:])
+        nc.scalar.activation(
+            neg_shift[:], soft_sum[:].bitcast(U32), ACT.Copy, scale=-SOFT * LN2 / 2.0**23, bias=SOFT * LN2 * 127.0
+        )
+        z = sb.tile([P, 1], F32, name="z")
+        nc.scalar.activation(p[:], a[:], ACT.Exp, bias=neg_shift[:], accum_out=z[:])
+        neg_row_term = sb.tile([P, 1], F32, name="neg_row_term")
+        nc.scalar.activation(neg_row_term[:], z[:], ACT.Copy, scale=neg_row_factor[:])
+
+        def grouped_view(tile, half):
+            return tile[:, half * HALF : (half + 1) * HALF].rearrange("p (g j) -> p g j", j=GROUP)
+
+        def spread(tile, half):
+            n = GROUPS // 2
+            return tile[:, half * n : (half + 1) * n].unsqueeze(2).to_broadcast([P, n, GROUP])
+
+        s = sb.tile([P, GROUPS], F32, name="s", tag="val_word_pool", align_bytes=64)
+        nc.vector.tensor_reduce(s[:], p[:].rearrange("p (g j) -> p g j", j=GROUP), AXIS.X, ALU.add)
+        den = sb.tile([P, GROUPS], F32, name="den", tag="gout_grouped", align_bytes=64)
+        nc.vector.tensor_scalar(den[:], s[:], group_factor[:], neg_row_term[:], ALU.mult, ALU.subtract)
+        inv = sb.tile([P, GROUPS], F32, name="inv")
+        nc.vector.reciprocal(inv[:], den[:])
+        weight = sb.tile([P, SLOTS], F32, name="weight")
+        direct = sb.tile([P, SLOTS], F32, name="direct")
+        u = sb.tile([P, GROUPS], F32, name="u")
+        for half in range(2):
+            nc.vector.tensor_tensor(grouped_view(weight, half), grouped_view(p, half), spread(inv, half), ALU.mult)
+        for half in range(2):
+            cols = slice(half * HALF, (half + 1) * HALF)
+            nc.vector.tensor_tensor(direct[:, cols], c0[:, cols], weight[:, cols], ALU.mult)
+        for half in range(2):
+            n = GROUPS // 2
+            nc.vector.tensor_reduce(u[:, half * n : (half + 1) * n], grouped_view(direct, half), AXIS.X, ALU.add)
+        row_parts = sb.tile([P, GROUPS], F32, name="row_parts")
+        dz = sb.tile([P, 1], F32, name="dz")
+        ds = sb.tile([P, GROUPS], F32, name="ds")
+        nc.vector.scalar_tensor_tensor(row_parts[:], u[:], neg_row_factor[:], inv[:], ALU.mult, ALU.mult, accum_out=dz[:])
+        nc.vector.scalar_tensor_tensor(ds[:], u[:], neg_group_factor[:], inv[:], ALU.mult, ALU.mult)
+        through = sb.tile([P, SLOTS], F32, name="through")
+        for half in range(2):
+            nc.vector.scalar_tensor_tensor(
+                grouped_view(through, half), spread(ds, half), dz[:], grouped_view(p, half), ALU.add, ALU.mult
+            )
+        for half in range(2):
+            cols = slice(half * HALF, (half + 1) * HALF)
+            listed = offsets[:, half * HALF // 16 : (half + 1) * HALF // 16]
+            nc.vector.tensor_tensor(placed[:].indirect(listed), direct[:, cols], through[:, cols], ALU.add)
+
+        start = 0
+        for width in STORE_WIDTHS:
+            cols = slice(start, start + width)
+            nc.vector.tensor_tensor(result[:, cols], result[:, cols], placed[:, cols], ALU.add)
+            nc.sync.dma_start(out[:, cols], result[:, cols])
+            start = start + width

@@ -25,20 +25,17 @@ GROUP_WEIGHT = 64.0
 SOFT = 4.0
 LN2 = 0.6931471805599453
 HALF = SLOTS // 2
-STORE_WIDTHS = (256, 256, 512, 512, 512)
+STORE_WIDTHS = (256, 512, 512, 512, 256)
 
 
 def tile_attend_bmixednorm_s_kernel(tc, query, keys_words, keys_scales, share, gout, vals_words, vals_scales, old, offs, out):
     nc = tc.nc
     with ExitStack() as ctx:
         sb = ctx.enter_context(tc.tile_pool(name="sb", bufs=1))
+        late = ctx.enter_context(tc.tile_pool(name="late", bufs=1))
         psum = ctx.enter_context(tc.psum_pool(name="psum", bufs=1))
 
-        offsets = sb.tile([P, SLOTS // 16], U16, name="offsets")
-        nc.sync.dma_start(offsets[:], offs)
-
-        def load_words(name, words):
-            word_pool = sb.tile([P, T], U16, name=name + "_word_pool", tag=name + "_word_pool", align_bytes=64)
+        def load_words(word_pool, words):
             nc.sync.dma_start(word_pool[:].bitcast(I32), words[0].bitcast(I32))
             return word_pool
 
@@ -52,8 +49,7 @@ def tile_attend_bmixednorm_s_kernel(tc, query, keys_words, keys_scales, share, g
                 )
             return scale_pool
 
-        def load_rows(name, rows):
-            raw = sb.tile([P, PACK, Q], F32, name=name + "_raw", tag="raw")
+        def load_rows(raw, rows):
             nc.sync.dma_start(raw[:], rows.rearrange("(p j) q -> p j q", j=PACK))
             return raw
 
@@ -67,34 +63,38 @@ def tile_attend_bmixednorm_s_kernel(tc, query, keys_words, keys_scales, share, g
             )
             return codes, code_scales
 
-        def gather(name, pool, dtype):
-            listed = sb.tile([P, SLOTS], dtype, name=name, align_bytes=64)
-            nc.vector.tensor_copy(listed[:], pool[:].indirect(offsets[:]))
+        def gather(listed, pool, first, count):
+            nc.vector.tensor_copy(listed[:], pool[:].indirect(offsets[:, first // 16 : (first + count) // 16]))
             return listed
 
-        def product(name, codes, code_scales, words, scales):
-            bank = psum.tile([P, SLOTS], F32, name=name + "_bank")
+        def product(bank, codes, code_scales, words, scales):
             nc.tensor.matmul_mx(
-                out=bank[:],
+                out=bank,
                 lhsT=codes[:].bitcast(FP8X4),
                 lhsT_scale=code_scales[:],
-                rhs=words[:].bitcast(FP4X4),
+                rhs=words.bitcast(FP4X4),
                 rhs_scale=scales[:],
                 start=True,
                 stop=True,
             )
-            return bank
 
-        key_word_pool = load_words("key", keys_words)
+        key_word_pool = load_words(sb.tile([P, T], U16, name="key_word_pool"), keys_words)
+        offsets = sb.tile([P, SLOTS // 16], U16, name="offsets")
+        nc.sync.dma_start(offsets[:], offs)
         key_scale_pool = load_scales("key", keys_scales)
-        share_col = sb.tile([P, 1], F32, name="share_col", tag="val_word_pool", align_bytes=64)
+        query_raw = load_rows(sb.tile([P, PACK, Q], F32, name="query_raw"), query)
+        share_col = sb.tile([P, 1], F32, name="share_col")
         nc.sync.dma_start(share_col[:], share)
-        query_raw = load_rows("query", query)
-        val_scale_pool = load_scales("val", vals_scales)
 
-        warm = sb.tile([P, 1], F32, name="warm")
+        warm = late.tile([P, 16], F32, name="warm", offset=2 * T - 32)
         nc.vector.memset(warm[:], 0.0)
         nc.scalar.activation(warm[:], warm[:], ACT.Exp)
+        gout_raw = load_rows(late.tile([P, PACK, Q], F32, name="gout_raw", offset=2 * T), gout)
+        val_word_pool = load_words(late.tile([P, T], U16, name="val_word_pool", offset=0), vals_words)
+
+        placed = sb.tile([P, T], F32, name="placed")
+        nc.vector.memset(placed[:].bitcast(I32), 0)
+        val_scale_pool = load_scales("val", vals_scales)
 
         group_factor = sb.tile([P, 1], F32, name="group_factor")
         neg_group_factor = sb.tile([P, 1], F32, name="neg_group_factor")
@@ -104,25 +104,22 @@ def tile_attend_bmixednorm_s_kernel(tc, query, keys_words, keys_scales, share, g
         nc.scalar.activation(neg_group_factor[:], share_col[:], ACT.Copy, scale=ratio, bias=-ratio)
         nc.scalar.activation(neg_row_factor[:], share_col[:], ACT.Copy, scale=-1.0 / OUT_SCALE)
 
-        val_word_pool = load_words("val", vals_words)
-        placed = sb.tile([P, T], F32, name="placed")
-        nc.vector.memset(placed[:], 0.0)
-
-        key_words = gather("key_words", key_word_pool, U16)
-        key_scales = gather("key_scales", key_scale_pool, U8)
+        key_words = gather(sb.tile([P, SLOTS], U16, name="key_words", align_bytes=64), key_word_pool, 0, SLOTS)
+        key_scales = gather(sb.tile([P, SLOTS], U8, name="key_scales", align_bytes=64), key_scale_pool, 0, SLOTS)
         query_codes, query_scales = quantise("query", query_raw)
-        a = product("score", query_codes, query_scales, key_words, key_scales)
+        a = psum.tile([P, SLOTS], F32, name="a")
+        product(a[:], query_codes, query_scales, key_words[:], key_scales)
 
-        gout_raw = load_rows("gout", gout)
-        val_scales = gather("val_scales", val_scale_pool, U8)
+        val_words = gather(sb.tile([P, SLOTS], U16, name="val_words", align_bytes=64), val_word_pool, 0, SLOTS)
         gout_codes, gout_scales = quantise("gout", gout_raw)
-        val_words = gather("val_words", val_word_pool, U16)
-        c0 = product("back", gout_codes, gout_scales, val_words, val_scales)
+        val_scales = gather(sb.tile([P, SLOTS], U8, name="val_scales", align_bytes=64), val_scale_pool, 0, SLOTS)
+        c0 = psum.tile([P, SLOTS], F32, name="c0")
+        product(c0[:], gout_codes, gout_scales, val_words[:], val_scales)
 
-        result = sb.tile([P, T], F32, name="result", tag="val_scale_pool", align_bytes=64)
+        result = sb.tile([P, T], F32, name="result", tag="key_scale_pool", align_bytes=64)
         nc.sync.dma_start(result[:], old)
 
-        p = sb.tile([P, SLOTS], F32, name="p")
+        p = late.tile([P, SLOTS], F32, name="p", offset=2 * T)
         soft_sum = sb.tile([P, 1], F32, name="soft_sum")
         neg_shift = sb.tile([P, 1], F32, name="neg_shift")
         nc.scalar.activation(p[:], a[:], ACT.Exp, scale=1.0 / SOFT, accum_out=soft_sum[:])
@@ -141,37 +138,53 @@ def tile_attend_bmixednorm_s_kernel(tc, query, keys_words, keys_scales, share, g
             n = GROUPS // 2
             return tile[:, half * n : (half + 1) * n].unsqueeze(2).to_broadcast([P, n, GROUP])
 
-        s = sb.tile([P, GROUPS], F32, name="s", tag="val_word_pool", align_bytes=64)
-        nc.vector.tensor_reduce(s[:], p[:].rearrange("p (g j) -> p g j", j=GROUP), AXIS.X, ALU.add)
+        def slots(half):
+            return slice(half * HALF, (half + 1) * HALF)
+
+        def groups(half):
+            return slice(half * GROUPS // 2, (half + 1) * GROUPS // 2)
+
+        s = sb.tile([P, GROUPS], F32, name="s", tag="val_scale_pool", align_bytes=64)
         den = sb.tile([P, GROUPS], F32, name="den", tag="gout_grouped", align_bytes=64)
-        nc.vector.tensor_scalar(den[:], s[:], group_factor[:], neg_row_term[:], ALU.mult, ALU.subtract)
         inv = sb.tile([P, GROUPS], F32, name="inv")
-        nc.vector.reciprocal(inv[:], den[:])
-        weight = sb.tile([P, SLOTS], F32, name="weight")
-        direct = sb.tile([P, SLOTS], F32, name="direct")
+        dvr = sb.tile([P, SLOTS], F32, name="dvr")
+        dv1 = sb.tile([P, GROUPS], F32, name="dv1")
         u = sb.tile([P, GROUPS], F32, name="u")
-        for half in range(2):
-            nc.vector.tensor_tensor(grouped_view(weight, half), grouped_view(p, half), spread(inv, half), ALU.mult)
-        for half in range(2):
-            cols = slice(half * HALF, (half + 1) * HALF)
-            nc.vector.tensor_tensor(direct[:, cols], c0[:, cols], weight[:, cols], ALU.mult)
-        for half in range(2):
-            n = GROUPS // 2
-            nc.vector.tensor_reduce(u[:, half * n : (half + 1) * n], grouped_view(direct, half), AXIS.X, ALU.add)
         row_parts = sb.tile([P, GROUPS], F32, name="row_parts")
         dz = sb.tile([P, 1], F32, name="dz")
         ds = sb.tile([P, GROUPS], F32, name="ds")
-        nc.vector.scalar_tensor_tensor(row_parts[:], u[:], neg_row_factor[:], inv[:], ALU.mult, ALU.mult, accum_out=dz[:])
-        nc.vector.scalar_tensor_tensor(ds[:], u[:], neg_group_factor[:], inv[:], ALU.mult, ALU.mult)
+        direct = sb.tile([P, SLOTS], F32, name="direct")
         through = sb.tile([P, SLOTS], F32, name="through")
-        for half in range(2):
-            nc.vector.scalar_tensor_tensor(
-                grouped_view(through, half), spread(ds, half), dz[:], grouped_view(p, half), ALU.add, ALU.mult
+
+        nc.vector.tensor_reduce(s[:], p[:].rearrange("p (g j) -> p g j", j=GROUP), AXIS.X, ALU.add)
+        nc.vector.tensor_tensor(dvr[:, slots(0)], c0[:, slots(0)], p[:, slots(0)], ALU.mult)
+        nc.vector.tensor_scalar(den[:], s[:], group_factor[:], neg_row_term[:], ALU.mult, ALU.subtract)
+        nc.vector.tensor_tensor(dvr[:, slots(1)], c0[:, slots(1)], p[:, slots(1)], ALU.mult)
+        nc.vector.reciprocal(inv[:], den[:])
+        nc.vector.tensor_reduce(dv1[:], dvr[:].rearrange("p (g j) -> p g j", j=GROUP), AXIS.X, ALU.add)
+        nc.vector.tensor_tensor(grouped_view(direct, 0), grouped_view(dvr, 0), spread(inv, 0), ALU.mult)
+        nc.vector.tensor_tensor(u[:], dv1[:], inv[:], ALU.mult)
+        quarter = HALF // 2
+        for part in range(2):
+            lo = HALF + part * quarter
+            nc.vector.tensor_tensor(
+                direct[:, lo : lo + quarter].rearrange("p (g j) -> p g j", j=GROUP),
+                dvr[:, lo : lo + quarter].rearrange("p (g j) -> p g j", j=GROUP),
+                inv[:, lo // GROUP : (lo + quarter) // GROUP].unsqueeze(2).to_broadcast([P, quarter // GROUP, GROUP]),
+                ALU.mult,
             )
-        for half in range(2):
-            cols = slice(half * HALF, (half + 1) * HALF)
-            listed = offsets[:, half * HALF // 16 : (half + 1) * HALF // 16]
-            nc.vector.tensor_tensor(placed[:].indirect(listed), direct[:, cols], through[:, cols], ALU.add)
+            if part == 0:
+                nc.vector.scalar_tensor_tensor(row_parts[:], u[:], neg_row_factor[:], inv[:], ALU.mult, ALU.mult, accum_out=dz[:])
+                nc.vector.scalar_tensor_tensor(ds[:], u[:], neg_group_factor[:], inv[:], ALU.mult, ALU.mult)
+        nc.vector.scalar_tensor_tensor(
+            through[:].rearrange("p (g j) -> p g j", j=GROUP),
+            ds[:].unsqueeze(2).to_broadcast([P, GROUPS, GROUP]),
+            dz[:],
+            p[:].rearrange("p (g j) -> p g j", j=GROUP),
+            ALU.add,
+            ALU.mult,
+        )
+        nc.vector.tensor_tensor(placed[:].indirect(offsets[:]), direct[:], through[:], ALU.add)
 
         start = 0
         for width in STORE_WIDTHS:

@@ -78,13 +78,11 @@ def tile_attend_bmixednorm_s_kernel(tc, query, keys_words, keys_scales, share, g
                 stop=True,
             )
 
-        key_word_pool = load_words(sb.tile([P, T], U16, name="key_word_pool"), keys_words)
         offsets = sb.tile([P, SLOTS // 16], U16, name="offsets")
         nc.sync.dma_start(offsets[:], offs)
+        key_word_pool = load_words(sb.tile([P, T], U16, name="key_word_pool"), keys_words)
         key_scale_pool = load_scales("key", keys_scales)
         query_raw = load_rows(sb.tile([P, PACK, Q], F32, name="query_raw"), query)
-        share_col = sb.tile([P, 1], F32, name="share_col")
-        nc.sync.dma_start(share_col[:], share)
 
         warm = late.tile([P, 16], F32, name="warm", offset=2 * T - 32)
         nc.vector.memset(warm[:], 0.0)
@@ -95,14 +93,6 @@ def tile_attend_bmixednorm_s_kernel(tc, query, keys_words, keys_scales, share, g
         placed = sb.tile([P, T], F32, name="placed")
         nc.vector.memset(placed[:].bitcast(I32), 0)
         val_scale_pool = load_scales("val", vals_scales)
-
-        group_factor = sb.tile([P, 1], F32, name="group_factor")
-        neg_group_factor = sb.tile([P, 1], F32, name="neg_group_factor")
-        neg_row_factor = sb.tile([P, 1], F32, name="neg_row_factor")
-        ratio = GROUP_WEIGHT / OUT_SCALE
-        nc.scalar.activation(group_factor[:], share_col[:], ACT.Copy, scale=-ratio, bias=ratio)
-        nc.scalar.activation(neg_group_factor[:], share_col[:], ACT.Copy, scale=ratio, bias=-ratio)
-        nc.scalar.activation(neg_row_factor[:], share_col[:], ACT.Copy, scale=-1.0 / OUT_SCALE)
 
         key_words = gather(sb.tile([P, SLOTS], U16, name="key_words", align_bytes=64), key_word_pool, 0, SLOTS)
         key_scales = gather(sb.tile([P, SLOTS], U8, name="key_scales", align_bytes=64), key_scale_pool, 0, SLOTS)
@@ -115,6 +105,16 @@ def tile_attend_bmixednorm_s_kernel(tc, query, keys_words, keys_scales, share, g
         val_scales = gather(sb.tile([P, SLOTS], U8, name="val_scales", align_bytes=64), val_scale_pool, 0, SLOTS)
         c0 = psum.tile([P, SLOTS], F32, name="c0")
         product(c0[:], gout_codes, gout_scales, val_words[:], val_scales)
+
+        share_col = sb.tile([P, 1], F32, name="share_col")
+        nc.gpsimd.dma_start(share_col[:], share)
+        group_factor = sb.tile([P, 1], F32, name="group_factor")
+        neg_group_factor = sb.tile([P, 1], F32, name="neg_group_factor")
+        neg_row_factor = sb.tile([P, 1], F32, name="neg_row_factor")
+        ratio = GROUP_WEIGHT / OUT_SCALE
+        nc.gpsimd.tensor_scalar(neg_row_factor[:], share_col[:], -1.0 / OUT_SCALE, 0.0, ALU.mult, ALU.add)
+        nc.gpsimd.tensor_scalar(group_factor[:], share_col[:], -ratio, ratio, ALU.mult, ALU.add)
+        nc.gpsimd.tensor_scalar(neg_group_factor[:], share_col[:], ratio, -ratio, ALU.mult, ALU.add)
 
         result = sb.tile([P, T], F32, name="result", tag="key_scale_pool", align_bytes=64)
         nc.sync.dma_start(result[:], old)

@@ -91,7 +91,8 @@ def tile_attend_bmixednorm_s_kernel(tc, query, keys_words, keys_scales, share, g
         val_word_pool = load_words(late.tile([P, T], U16, name="val_word_pool", offset=0), vals_words)
 
         placed = sb.tile([P, T], F32, name="placed")
-        nc.vector.memset(placed[:].bitcast(I32), 0)
+        nc.vector.memset(placed[:, :1280].bitcast(I32), 0)
+        nc.gpsimd.memset(placed[:, 1280:].bitcast(I32), 0)
         val_scale_pool = load_scales("val", vals_scales)
 
         key_words = gather(sb.tile([P, SLOTS], U16, name="key_words", align_bytes=64), key_word_pool, 0, SLOTS)

from contextlib import ExitStack

import concourse.mybir as mybir

D, E, T, SLOTS, Q, GROUPS = 512, 512, 2048, 512, 128, 64
GROUP = SLOTS // GROUPS
P = 128
PACK = 4
FLOPS = 2 * Q * SLOTS * (D + E)

F32 = mybir.dt.float32
BF16 = mybir.dt.bfloat16
I32 = mybir.dt.int32
U32 = mybir.dt.uint32
U16 = mybir.dt.uint16
U8 = mybir.dt.uint8
FP8X4 = mybir.dt.float8_e4m3fn_x4
FP4X4 = mybir.dt.float4_e2m1fn_x4
ALU = mybir.AluOpType
ACT = mybir.ActivationFunctionType
AXIS = mybir.AxisListType

OUT_SCALE = 512.0
GROUP_WEIGHT = 64.0
SOFT = 4.0
LN2 = 0.6931471805599453
HALF = SLOTS // 2
STORE_WIDTHS = (256, 512, 512, 512, 256)


def tile_attend_bmixednorm_s_kernel(tc, query, keys_words, keys_scales, share, gout, vals_words, vals_scales, old, offs, out):
    nc = tc.nc
    with ExitStack() as ctx:
        sb = ctx.enter_context(tc.tile_pool(name="sb", bufs=1))
        late = ctx.enter_context(tc.tile_pool(name="late", bufs=1))
        psum = ctx.enter_context(tc.psum_pool(name="psum", bufs=1))

        def load_words(word_pool, words):
            nc.sync.dma_start(word_pool[:].bitcast(I32), words[0].bitcast(I32))
            return word_pool

        def load_scales(name, scales):
            scale_pool = sb.tile([P, T], U8, name=name + "_scale_pool", tag=name + "_scale_pool", align_bytes=64)
            nc.vector.memset(scale_pool[:].bitcast(I32), 0)
            for quadrant in range(4):
                nc.sync.dma_start(
                    scale_pool[32 * quadrant : 32 * quadrant + 4, :].bitcast(I32),
                    scales[0, 4 * quadrant : 4 * quadrant + 4, :].bitcast(I32),
                )
            return scale_pool

        def load_rows(raw, rows):
            nc.sync.dma_start(raw[:], rows.rearrange("(p j) q -> p j q", j=PACK))
            return raw

        def quantise(name, raw):
            grouped = sb.tile([P, Q, PACK], BF16, name=name + "_grouped", tag=name + "_grouped", align_bytes=64)
            nc.scalar.copy(grouped[:], raw[:].rearrange("p j q -> p q j"))
            codes = sb.tile([P, Q], U32, name=name + "_codes", align_bytes=64)
            code_scales = sb.tile([P, Q], U8, name=name + "_code_scales", align_bytes=64)
            nc.vector.quantize_mx(
                out=codes[:].bitcast(FP8X4), scales=code_scales[:], in_=grouped[:].rearrange("p q j -> p (q j)")
            )
            return codes, code_scales

        def gather(listed, pool, first, count):
            nc.vector.tensor_copy(listed[:], pool[:].indirect(offsets[:, first // 16 : (first + count) // 16]))
            return listed

        def product(bank, codes, code_scales, words, scales):
            nc.tensor.matmul_mx(
                out=bank,
                lhsT=codes[:].bitcast(FP8X4),
                lhsT_scale=code_scales[:],
                rhs=words.bitcast(FP4X4),
                rhs_scale=scales[:],
                start=True,
                stop=True,
            )

        offsets = sb.tile([P, SLOTS // 16], U16, name="offsets")
        nc.sync.dma_start(offsets[:], offs)
        key_word_pool = load_words(sb.tile([P, T], U16, name="key_word_pool"), keys_words)
        key_scale_pool = load_scales("key", keys_scales)
        query_raw = load_rows(sb.tile([P, PACK, Q], F32, name="query_raw"), query)

        warm = late.tile([P, 16], F32, name="warm", offset=2 * T - 32)
        nc.vector.memset(warm[:], 0.0)
        nc.scalar.activation(warm[:], warm[:], ACT.Exp)
        gout_raw = load_rows(late.tile([P, PACK, Q], F32, name="gout_raw", offset=2 * T), gout)
        val_word_pool = load_words(late.tile([P, T], U16, name="val_word_pool", offset=0), vals_words)

        placed = sb.tile([P, T], F32, name="placed")
        nc.vector.memset(placed[:, :1280].bitcast(I32), 0)
        nc.gpsimd.memset(placed[:, 1280:].bitcast(I32), 0)
        val_scale_pool = load_scales("val", vals_scales)

        key_words = gather(sb.tile([P, SLOTS], U16, name="key_words", align_bytes=64), key_word_pool, 0, SLOTS)
        key_scales = gather(sb.tile([P, SLOTS], U8, name="key_scales", align_bytes=64), key_scale_pool, 0, SLOTS)
        query_codes, query_scales = quantise("query", query_raw)
        a = psum.tile([P, SLOTS], F32, name="a")
        product(a[:], query_codes, query_scales, key_words[:], key_scales)

        val_words = gather(sb.tile([P, SLOTS], U16, name="val_words", align_bytes=64), val_word_pool, 0, SLOTS)
        gout_codes, gout_scales = quantise("gout", gout_raw)
        val_scales = gather(sb.tile([P, SLOTS], U8, name="val_scales", align_bytes=64), val_scale_pool, 0, SLOTS)
        c0 = psum.tile([P, SLOTS], F32, name="c0")
        product(c0[:], gout_codes, gout_scales, val_words[:], val_scales)

        share_col = sb.tile([P, 1], F32, name="share_col")
        nc.gpsimd.dma_start(share_col[:], share)
        group_factor = sb.tile([P, 1], F32, name="group_factor")
        neg_group_factor = sb.tile([P, 1], F32, name="neg_group_factor")
        neg_row_factor = sb.tile([P, 1], F32, name="neg_row_factor")
        ratio = GROUP_WEIGHT / OUT_SCALE
        nc.gpsimd.tensor_scalar(neg_row_factor[:], share_col[:], -1.0 / OUT_SCALE, 0.0, ALU.mult, ALU.add)
        nc.gpsimd.tensor_scalar(group_factor[:], share_col[:], -ratio, ratio, ALU.mult, ALU.add)
        nc.gpsimd.tensor_scalar(neg_group_factor[:], share_col[:], ratio, -ratio, ALU.mult, ALU.add)

        result = sb.tile([P, T], F32, name="result", tag="key_scale_pool", align_bytes=64)
        nc.sync.dma_start(result[:], old)

        p = late.tile([P, SLOTS], F32, name="p", offset=2 * T)
        soft_sum = sb.tile([P, 1], F32, name="soft_sum")
        neg_shift = sb.tile([P, 1], F32, name="neg_shift")
        nc.scalar.activation(p[:], a[:], ACT.Exp, scale=1.0 / SOFT, accum_out=soft_sum[:])
        nc.scalar.activation(
            neg_shift[:], soft_sum[:].bitcast(U32), ACT.Copy, scale=-SOFT * LN2 / 2.0**23, bias=SOFT * LN2 * 127.0
        )
        z = sb.tile([P, 1], F32, name="z")
        nc.scalar.activation(p[:], a[:], ACT.Exp, bias=neg_shift[:], accum_out=z[:])
        neg_row_term = sb.tile([P, 1], F32, name="neg_row_term")
        nc.scalar.activation(neg_row_term[:], z[:], ACT.Copy, scale=neg_row_factor[:])

        def grouped_view(tile, half):
            return tile[:, half * HALF : (half + 1) * HALF].rearrange("p (g j) -> p g j", j=GROUP)

        def spread(tile, half):
            n = GROUPS // 2
            return tile[:, half * n : (half + 1) * n].unsqueeze(2).to_broadcast([P, n, GROUP])

        def slots(half):
            return slice(half * HALF, (half + 1) * HALF)

        def groups(half):
            return slice(half * GROUPS // 2, (half + 1) * GROUPS // 2)

        s = sb.tile([P, GROUPS], F32, name="s", tag="val_scale_pool", align_bytes=64)
        den = sb.tile([P, GROUPS], F32, name="den", tag="gout_grouped", align_bytes=64)
        inv = sb.tile([P, GROUPS], F32, name="inv")
        dvr = sb.tile([P, SLOTS], F32, name="dvr")
        dv1 = sb.tile([P, GROUPS], F32, name="dv1")
        u = sb.tile([P, GROUPS], F32, name="u")
        row_parts = sb.tile([P, GROUPS], F32, name="row_parts")
        dz = sb.tile([P, 1], F32, name="dz")
        ds = sb.tile([P, GROUPS], F32, name="ds")
        direct = sb.tile([P, SLOTS], F32, name="direct")
        through = sb.tile([P, SLOTS], F32, name="through")

        nc.vector.tensor_reduce(s[:], p[:].rearrange("p (g j) -> p g j", j=GROUP), AXIS.X, ALU.add)
        nc.vector.tensor_tensor(dvr[:, slots(0)], c0[:, slots(0)], p[:, slots(0)], ALU.mult)
        nc.vector.tensor_scalar(den[:], s[:], group_factor[:], neg_row_term[:], ALU.mult, ALU.subtract)
        nc.vector.tensor_tensor(dvr[:, slots(1)], c0[:, slots(1)], p[:, slots(1)], ALU.mult)
        nc.vector.reciprocal(inv[:], den[:])
        nc.vector.tensor_reduce(dv1[:], dvr[:].rearrange("p (g j) -> p g j", j=GROUP), AXIS.X, ALU.add)
        nc.vector.tensor_tensor(grouped_view(direct, 0), grouped_view(dvr, 0), spread(inv, 0), ALU.mult)
        nc.vector.tensor_tensor(u[:], dv1[:], inv[:], ALU.mult)
        quarter = HALF // 2
        for part in range(2):
            lo = HALF + part * quarter
            nc.vector.tensor_tensor(
                direct[:, lo : lo + quarter].rearrange("p (g j) -> p g j", j=GROUP),
                dvr[:, lo : lo + quarter].rearrange("p (g j) -> p g j", j=GROUP),
                inv[:, lo // GROUP : (lo + quarter) // GROUP].unsqueeze(2).to_broadcast([P, quarter // GROUP, GROUP]),
                ALU.mult,
            )
            if part == 0:
                nc.vector.scalar_tensor_tensor(row_parts[:], u[:], neg_row_factor[:], inv[:], ALU.mult, ALU.mult, accum_out=dz[:])
                nc.vector.scalar_tensor_tensor(ds[:], u[:], neg_group_factor[:], inv[:], ALU.mult, ALU.mult)
        nc.vector.scalar_tensor_tensor(
            through[:].rearrange("p (g j) -> p g j", j=GROUP),
            ds[:].unsqueeze(2).to_broadcast([P, GROUPS, GROUP]),
            dz[:],
            p[:].rearrange("p (g j) -> p g j", j=GROUP),
            ALU.add,
            ALU.mult,
        )
        nc.vector.tensor_tensor(placed[:].indirect(offsets[:]), direct[:], through[:], ALU.add)

        start = 0
        for width in STORE_WIDTHS:
            cols = slice(start, start + width)
            nc.vector.tensor_tensor(result[:, cols], result[:, cols], placed[:, cols], ALU.add)
            nc.sync.dma_start(out[:, cols], result[:, cols])
            start = start + width
